import numpy as np
import ml_dtypes


def mxq(x, axis, fmt="e4m3"):
    dtype, down = {"e4m3": (ml_dtypes.float8_e4m3fn, 7), "e5m2": (ml_dtypes.float8_e5m2, 14)}[fmt]
    v = np.moveaxis(np.asarray(x, np.float32).astype(ml_dtypes.bfloat16).astype(np.float64), axis, -1)
    blocks = v.reshape(v.shape[:-1] + (-1, 32))
    amax = np.abs(blocks).max(-1, keepdims=True)
    byte = np.maximum(np.where(amax > 0, np.frexp(amax)[1] - 1 + 127, 0) - down, 1)
    scale = np.exp2(byte - 127.0)
    codes = (blocks / scale).astype(np.float32).astype(dtype).astype(np.float64)
    return np.moveaxis((codes * scale).reshape(v.shape), -1, axis)


WIDE = False


def mx_kscale(k):
    if not WIDE:
        return np.ones(k)
    levels = np.array([10, -10, 5, -5, 0])
    if k % 512:
        return np.exp2(np.random.permutation(np.resize(levels, k // 32))).repeat(32)
    a = np.empty((k // 512, 16))
    for p in range(k // 512):
        a[p, :8] = np.random.permutation(np.resize(levels, 8))
        for g in range(8):
            far = levels[np.abs(levels - a[p, g]) >= 10]
            a[p, g + 8] = far[np.random.randint(len(far))]
    return np.exp2(a.ravel()).repeat(32)


def f64(x):
    return np.asarray(x).astype(np.float64)


def striped(idx):
    return np.tile(idx.reshape(-1, 16).T, (8, 1)).astype(np.uint16)


def unstriped(offs):
    return offs[:16].T.reshape(-1).astype(np.int64)


def pack_weight(w):
    k, n = w.shape
    w = f64(np.asarray(w, np.float32).astype(ml_dtypes.bfloat16)).reshape(k // 32, 32, n)
    amax = np.abs(w).max(1)
    byte = np.clip(np.where(amax > 0, np.frexp(amax)[1] - 1 + 127 - 7, 1), 1, 254)
    scaled = (w * np.exp2(127.0 - byte)[:, None, :]).reshape(k, n).astype(np.float32)
    words = np.ascontiguousarray(scaled.reshape(k // 512, 128, 4, n).transpose(0, 1, 3, 2)).astype(ml_dtypes.float8_e4m3fn).view(np.uint8)
    return words, np.ascontiguousarray(byte.astype(np.uint8).reshape(k // 512, 16, n))


def unpack_weight(words, scales):
    g, p, n, _ = words.shape
    vals = np.ascontiguousarray(words).view(ml_dtypes.float8_e4m3fn).astype(np.float64) * np.repeat(np.exp2(scales.astype(np.float64) - 127.0), 8, axis=1)[..., None]
    return vals.transpose(0, 1, 3, 2).reshape(g * 512, n)


E2M1 = np.array([0.0, 0.5, 1.0, 1.5, 2.0, 3.0, 4.0, 6.0, -0.0, -0.5, -1.0, -1.5, -2.0, -3.0, -4.0, -6.0])


def pack_fp4(w):
    k, n = w.shape
    w = f64(np.asarray(w, np.float32).astype(ml_dtypes.bfloat16)).reshape(k // 32, 32, n)
    amax = np.abs(w).max(1)
    mant, ex = np.frexp(amax / 6.0)
    byte = np.clip(np.where(amax > 0, np.where(mant > 0.5, ex, ex - 1) + 127, 1), 1, 254)
    scaled = (w * np.exp2(127.0 - byte)[:, None, :]).reshape(k, n).astype(np.float32)
    c = np.ascontiguousarray(scaled.reshape(k // 512, 128, 4, n).transpose(0, 1, 3, 2)).astype(ml_dtypes.float4_e2m1fn).view(np.uint8) & 0xF
    words = (c[..., 0::2] | (c[..., 1::2] << 4)).reshape(k // 512, 128, 2 * n)
    return np.ascontiguousarray(words), np.ascontiguousarray(byte.astype(np.uint8).reshape(k // 512, 16, n))


def unpack_fp4(words, scales):
    g, _, n = scales.shape
    words = np.ascontiguousarray(words).reshape(g, 128, n, 2)
    nib = np.empty((g, 128, n, 4), np.uint8)
    nib[..., 0::2] = words & 0xF
    nib[..., 1::2] = words >> 4
    vals = E2M1[nib] * np.repeat(np.exp2(scales.astype(np.float64) - 127.0), 8, axis=1)[..., None]
    return vals.transpose(0, 1, 3, 2).reshape(g * 512, n)


def planes(y):
    n, m = y.shape
    v = y.astype(np.float32).astype(ml_dtypes.bfloat16).astype(np.float64).reshape(n // 32, 32, m)
    top = np.abs(v).max(1)
    byte = np.clip(np.where(top > 0, np.frexp(top)[1] - 1 + 127 - 7, 1), 1, 254)
    codes = (v * np.exp2(127.0 - byte)[:, None, :]).reshape(n, m).astype(np.float32).astype(ml_dtypes.float8_e4m3fn).view(np.uint8)
    words = codes.reshape(n // 512, 128, 4, m).transpose(0, 1, 3, 2)
    return np.ascontiguousarray(words), np.ascontiguousarray(byte.astype(np.uint8).reshape(n // 512, 16, m))


K, T, S, H, Z, W = 512, 2048, 512, 512, 512, 2048


def setup_inputs():
    n = np.random.standard_normal
    s = mx_kscale(K)[:, None]
    u = mx_kscale(H)
    packed_xT = pack_weight(n((K, T)) * s)
    packed_w1 = pack_fp4(n((K, H)) / np.sqrt(K) / s)
    packed_eT = pack_weight(n((K, W)) * s)
    packed_w2 = pack_fp4(n((K, H)) / np.sqrt(K) / s)
    return {
        "x_words": packed_xT[0],
        "x_scales": packed_xT[1],
        "w1_words": packed_w1[0],
        "w1_scales": packed_w1[1],
        "e_words": packed_eT[0],
        "e_scales": packed_eT[1],
        "w2_words": packed_w2[0],
        "w2_scales": packed_w2[1],
        "unit": (np.random.uniform(0.6, 1.4, (H, 1)) * u[:, None]).astype(np.float32),
        "unit2": (np.random.uniform(0.6, 1.4, (H, 1)) / np.sqrt(H) / u[:, None]).astype(np.float32),
        "offs": striped(np.random.permutation(T)[:S]),
        "col_": striped(np.random.permutation(W)[:Z]),
        "gr": striped(np.random.permutation(S)),
        "gc": striped(np.random.permutation(Z)),
        "pair": striped(np.random.permutation(Z)),
    }


def reference(x_words, x_scales, w1_words, w1_scales, e_words, e_scales, w2_words, w2_scales, unit, unit2, offs, col_, gr, gc, pair):
    xq = unpack_weight(x_words, x_scales)[:, unstriped(offs)]
    y = unpack_fp4(w1_words, w1_scales).T @ xq
    yg_ = y[:, unstriped(gr)]
    rsm = 0.5 * (y + yg_)
    hid = f64(unit) * rsm
    e_col_ = unpack_weight(e_words, e_scales)[:, unstriped(col_)]
    ye = unpack_fp4(w2_words, w2_scales).T @ e_col_
    eg = ye[:, unstriped(gc)]
    csm = 0.5 * (ye + eg)
    hid2 = f64(unit2) * csm
    sc = mxq(hid, 0, "e4m3").T @ mxq(hid2, 0, "e4m3")
    rmu = sc.mean(axis=1, keepdims=True)
    res = sc - rmu
    absx = np.abs(res)
    mad = absx.mean(axis=1, keepdims=True)
    z_ = res / (mad + 0.2)
    out_0 = np.maximum(z_, -1.0 * z_[:, unstriped(pair)])
    return (out_0,) + planes(out_0)

@@ -1,0 +1,278 @@
+from contextlib import ExitStack
+
+import concourse.mybir as mybir
+
+K, T, S, H = 512, 2048, 512, 512
+FLOPS = 3 * 2 * 512 * 512 * 512
+BYTES = 2 * (S * 512 + S * 16) + 2 * (128 * 1024 + 16 * 512) + 2 * 2048 + 5 * 4096 + 512 * 512 * 4 + 512 * 512 + 16 * 512
+
+F32 = mybir.dt.float32
+BF16 = mybir.dt.bfloat16
+I32 = mybir.dt.int32
+U32 = mybir.dt.uint32
+U16 = mybir.dt.uint16
+U8 = mybir.dt.uint8
+FP8X4 = mybir.dt.float8_e4m3fn_x4
+FP4X4 = mybir.dt.float4_e2m1fn_x4
+ACT = mybir.ActivationFunctionType
+ALU = mybir.AluOpType
+
+P = 128
+PACK = 4
+HALF = S // 2
+LIST_COLS = S // 16
+
+
+def tile_picked_ycoclus_max_po_kernel(
+    tc, x_words, x_scales, w1_words, w1_scales, e_words, e_scales, w2_words, w2_scales,
+    unit, unit2, offs, col_, gr, gc, pair, out_0, out_1, out_2,
+):
+    nc = tc.nc
+    with ExitStack() as ctx:
+        keep = ctx.enter_context(tc.tile_pool(name="keep", bufs=1))
+        psum = ctx.enter_context(tc.psum_pool(name="psum", bufs=1))
+
+        def load_list(name, src):
+            tile = keep.tile([P, LIST_COLS], U16, name=name)
+            nc.sync.dma_start(tile[:], src)
+            return tile
+
+        def load_scale_rows(queue, plane, src):
+            for q in range(4):
+                queue.dma_start(plane[32 * q : 32 * q + 4, :].bitcast(I32), src[0, 4 * q : 4 * q + 4, :].bitcast(I32))
+
+        def fill_scale_rows(queue, plane, src):
+            for q in range(4):
+                rows = src[0, 4 * q : 4 * q + 4, :].bitcast(I32)
+                queue.dma_start(
+                    plane[32 * q : 32 * q + 32, :].bitcast(I32),
+                    rows.unsqueeze(0).to_broadcast([8, 4, rows.shape[1]]),
+                )
+
+        x_plane = keep.tile([P, T], U8, name="x_plane", align_bytes=64)
+        e_plane = keep.tile([P, T], U8, name="e_plane", tag="e_plane", align_bytes=64)
+        w1_plane = keep.tile([P, H], U8, name="w1_plane", align_bytes=64)
+        w2_plane = keep.tile([P, H], U8, name="w2_plane", align_bytes=64)
+        nc.gpsimd.memset(e_plane[:].bitcast(I32), 0)
+
+        x_table = keep.tile([P, T], U32, name="x_table", tag="x_table", align_bytes=64)
+        e_table = keep.tile([P, T], U32, name="e_table", align_bytes=64)
+        w1_raw = keep.tile([P, 2 * H], U8, name="w1_raw", align_bytes=64)
+        w2_raw = keep.tile([P, 2 * H], U8, name="w2_raw", align_bytes=64)
+        u1 = keep.tile([P, PACK], F32, name="u1")
+        u2 = keep.tile([P, PACK], F32, name="u2")
+
+        fill_scale_rows(nc.sync, x_plane, x_scales)
+        offs_t = load_list("offs_t", offs)
+        nc.sync.dma_start(w1_raw[:].bitcast(I32), w1_words[0].bitcast(I32))
+        nc.sync.dma_start(x_table[:].bitcast(I32), x_words[0].rearrange("p n t -> p (n t)").bitcast(I32))
+        fill_scale_rows(nc.sync, w1_plane, w1_scales)
+        nc.sync.dma_start(u1[:], unit.rearrange("(p t) o -> p (t o)", t=PACK))
+        col_t = load_list("col_t", col_)
+        nc.sync.dma_start(e_table[:].bitcast(I32), e_words[0].rearrange("p n t -> p (n t)").bitcast(I32))
+        load_scale_rows(nc.gpsimd, e_plane, e_scales)
+        nc.sync.dma_start(w2_raw[:].bitcast(I32), w2_words[0].bitcast(I32))
+        fill_scale_rows(nc.sync, w2_plane, w2_scales)
+        gr_t = load_list("gr_t", gr)
+        nc.sync.dma_start(u2[:], unit2.rearrange("(p t) o -> p (t o)", t=PACK))
+        gc_t = load_list("gc_t", gc)
+        pair_t = load_list("pair_t", pair)
+
+        half_u1 = keep.tile([P, PACK], F32, name="half_u1")
+        half_u2 = keep.tile([P, PACK], F32, name="half_u2", tag="half_u2", align_bytes=64)
+        nc.scalar.activation(half_u1[:], u1[:], ACT.Copy, scale=0.5)
+        nc.scalar.activation(half_u2[:], u2[:], ACT.Copy, scale=0.5)
+
+        def deal_words(name, raw):
+            words = keep.tile([P, 2 * H], U8, name=name + "_words", align_bytes=64)
+            nc.vector.tensor_copy(
+                words[:].rearrange("p (t m b) -> p m t b", t=PACK, b=2),
+                raw[:].rearrange("p (m t b) -> p m t b", t=PACK, b=2),
+            )
+            return words
+
+        def deal_scales(name, plane):
+            scales = keep.tile([P, H], U8, name=name + "_scales", align_bytes=64)
+            nc.vector.tensor_copy(
+                scales[:].rearrange("p (t m) -> p m t", t=PACK),
+                plane[:].rearrange("p (m t) -> p m t", t=PACK),
+            )
+            return scales
+
+        def pick(name, dtype, table, entries, tag):
+            picked = keep.tile([P, S], dtype, name=name, tag=tag, align_bytes=64)
+            nc.vector.tensor_copy(picked[:], table[:].indirect(entries[:]))
+            return picked
+
+        banks = [psum.tile([P, S], F32, name="bank%d" % b) for b in range(8)]
+
+        def first_product(bank4, w_words, w_scales, words, scales):
+            for t in range(PACK):
+                nc.tensor.matmul_mx(
+                    out=bank4[t][:],
+                    lhsT=w_words[:, 2 * P * t : 2 * P * (t + 1)].bitcast(FP4X4),
+                    lhsT_scale=w_scales[:, P * t : P * (t + 1)],
+                    rhs=words[:].bitcast(FP8X4),
+                    rhs_scale=scales[:],
+                    start=True,
+                    stop=True,
+                )
+
+        x_sc = pick("x_sc", U8, x_plane, offs_t, "x_sc")
+        w1_w = deal_words("w1", w1_raw)
+        x_w = pick("x_w", U32, x_table, offs_t, "x_w")
+        w1_s = deal_scales("w1", w1_plane)
+        first_product(banks[:4], w1_w, w1_s, x_w, x_sc)
+        e_sc = pick("e_sc", U8, e_plane, col_t, "x_table")
+        e_w = pick("e_w", U32, e_table, col_t, "e_plane")
+        w2_w = deal_words("w2", w2_raw)
+        w2_s = deal_scales("w2", w2_plane)
+        first_product(banks[4:], w2_w, w2_s, e_w, e_sc)
+
+        def half_of(entries, h):
+            return entries[:, h * LIST_COLS // 2 : (h + 1) * LIST_COLS // 2]
+
+        def gather(engine, dst, window, entries):
+            if engine == "scalar":
+                nc.scalar.activation(dst, window.indirect(entries), ACT.Copy)
+            else:
+                nc.vector.tensor_copy(dst, window.indirect(entries))
+
+        y = keep.tile([P, PACK, S], F32, name="y", align_bytes=64)
+        ye = keep.tile([P, PACK, S], F32, name="ye", align_bytes=64)
+        yg = [keep.tile([P, PACK, HALF], F32, name="yg%d" % h, align_bytes=64) for h in range(2)]
+        eg = [keep.tile([P, PACK, HALF], F32, name="eg%d" % h, align_bytes=64) for h in range(2)]
+        hid = keep.tile([P, PACK, P, PACK], BF16, name="hid", tag="half_u2", align_bytes=64)
+        hid2 = [keep.tile([P, HALF, PACK], BF16, name="hid2_%d" % h, align_bytes=64) for h in range(2)]
+        hid_w = keep.tile([P, S], U32, name="hid_w", align_bytes=64)
+        hid_s = keep.tile([P, S], U8, name="hid_s", align_bytes=64)
+        hid2_w = [keep.tile([P, HALF], U32, name="hid2_w%d" % h, align_bytes=64) for h in range(2)]
+        hid2_s = [keep.tile([P, HALF], U8, name="hid2_s%d" % h, align_bytes=64) for h in range(2)]
+
+        def sum_rows(h):
+            m = slice(h * P // 2, (h + 1) * P // 2)
+            nc.vector.tensor_tensor(
+                hid[:, :, m, :].rearrange("p s m t -> p m t s"),
+                yg[h][:].rearrange("p t (m s) -> p m t s", s=PACK),
+                y[:, :, h * HALF : (h + 1) * HALF].rearrange("p t (m s) -> p m t s", s=PACK),
+                ALU.add,
+            )
+
+        def sum_cols(h):
+            nc.vector.tensor_tensor(
+                hid2[h][:].rearrange("p (c i) t -> p c t i", i=4),
+                eg[h][:].rearrange("p t (c i) -> p c t i", i=4),
+                ye[:, :, h * HALF : (h + 1) * HALF].rearrange("p t (c i) -> p c t i", i=4),
+                ALU.add,
+            )
+
+        def quant_cols(h):
+            nc.vector.quantize_mx(
+                out=hid2_w[h][:].bitcast(FP8X4), scales=hid2_s[h][:], in_=hid2[h][:].rearrange("p e t -> p (e t)")
+            )
+
+        def second_product(h):
+            for s in range(PACK):
+                nc.tensor.matmul_mx(
+                    out=banks[s][:, h * HALF : (h + 1) * HALF],
+                    lhsT=hid_w[:, P * s : P * (s + 1)].bitcast(FP8X4),
+                    lhsT_scale=hid_s[:, P * s : P * (s + 1)],
+                    rhs=hid2_w[h][:].bitcast(FP8X4),
+                    rhs_scale=hid2_s[h][:],
+                    start=True,
+                    stop=True,
+                )
+
+        neg = keep.tile([P, PACK, S], F32, name="neg", align_bytes=64)
+        dev = keep.tile([P, S], F32, name="dev", align_bytes=64)
+        neg_sum = [[keep.tile([P, 1], F32, name="neg_sum%d_%d" % (s, h)) for h in range(2)] for s in range(PACK)]
+        dev_sum = [keep.tile([P, 1], F32, name="dev_sum%d" % s) for s in range(PACK)]
+        two_mu = [keep.tile([P, 1], F32, name="two_mu%d" % s) for s in range(PACK)]
+        neg_mu = [keep.tile([P, 1], F32, name="neg_mu%d" % s) for s in range(PACK)]
+        den = [keep.tile([P, 1], F32, name="den%d" % s) for s in range(PACK)]
+        inv = [keep.tile([P, 1], F32, name="inv%d" % s) for s in range(PACK)]
+        ng = [keep.tile([P, PACK, HALF], F32, name="ng%d" % h, align_bytes=64) for h in range(2)]
+        top = [keep.tile([P, PACK, HALF], F32, name="top%d" % h, align_bytes=64) for h in range(2)]
+        res = [keep.tile([P, PACK, HALF], F32, name="res%d" % h, align_bytes=64) for h in range(2)]
+        res_b = [keep.tile([P, HALF, PACK], BF16, name="res_b%d" % h, align_bytes=64) for h in range(2)]
+        res_w = [keep.tile([P, HALF], U32, name="res_w%d" % h, align_bytes=64) for h in range(2)]
+        res_s = keep.tile([P, S], U8, name="res_s", align_bytes=64)
+        out_rows = out_0.rearrange("(p s) e -> p s e", s=PACK)
+        out_words = out_1[0].rearrange("p e t -> p (e t)").bitcast(I32)
+
+        def negate(s, h):
+            cols = slice(h * HALF, (h + 1) * HALF)
+            nc.scalar.activation(neg[:, s, cols], banks[s][:, cols], ACT.Copy, scale=-1.0, accum_out=neg_sum[s][h][:])
+
+        def means(s):
+            nc.gpsimd.tensor_scalar(neg_mu[s][:], neg_sum[s][0][:], neg_sum[s][1][:], 1.0 / S, ALU.add, ALU.mult)
+            nc.gpsimd.tensor_scalar(two_mu[s][:], neg_sum[s][0][:], neg_sum[s][1][:], -2.0 / S, ALU.add, ALU.mult)
+
+        def spread(s):
+            nc.scalar.activation(dev[:], banks[s][:], ACT.Abs, bias=neg_mu[s][:], accum_out=dev_sum[s][:])
+            nc.gpsimd.tensor_scalar(den[s][:], dev_sum[s][:], 1.0 / S, 0.2, ALU.mult, ALU.add)
+
+        def finish(s, h):
+            cols = slice(h * HALF, (h + 1) * HALF)
+            nc.vector.scalar_tensor_tensor(
+                top[h][:, s, :], ng[h][:, s, :], two_mu[s][:], banks[s][:, cols], ALU.add, ALU.max
+            )
+            if h == 0:
+                nc.vector.reciprocal(inv[s][:], den[s][:])
+            nc.vector.tensor_scalar(res[h][:, s, :], top[h][:, s, :], neg_mu[s][:], inv[s][:], ALU.add, ALU.mult)
+            nc.sync.dma_start(out_rows[:, s, cols], res[h][:, s, :])
+
+        def hand_on(h):
+            cols = slice(h * HALF, (h + 1) * HALF)
+            nc.vector.tensor_copy(
+                res_b[h][:].rearrange("p (c i) t -> p c t i", i=4),
+                res[h][:].rearrange("p t (c i) -> p c t i", i=4),
+            )
+            nc.vector.quantize_mx(
+                out=res_w[h][:].bitcast(FP8X4), scales=res_s[:, cols], in_=res_b[h][:].rearrange("p e t -> p (e t)")
+            )
+            nc.sync.dma_start(out_words[:, cols], res_w[h][:].bitcast(I32))
+
+        for t in range(PACK):
+            nc.scalar.activation(y[:, t, :], banks[t][:], ACT.Copy, scale=half_u1[:, t : t + 1])
+        for t in range(PACK):
+            gather("scalar", yg[0][:, t, :], y[:, t, :], half_of(gr_t, 0))
+        for t in range(PACK):
+            nc.vector.tensor_scalar(ye[:, t, :], banks[4 + t][:], half_u2[:, t : t + 1], None, ALU.mult)
+        for t in range(PACK):
+            gather("scalar", yg[1][:, t, :], y[:, t, :], half_of(gr_t, 1))
+        sum_rows(0)
+        for t in range(PACK):
+            gather("vector" if t < 1 else "scalar", eg[0][:, t, :], ye[:, t, :], half_of(gc_t, 0))
+        sum_rows(1)
+        for t in range(PACK):
+            gather("scalar", eg[1][:, t, :], ye[:, t, :], half_of(gc_t, 1))
+        sum_cols(0)
+        nc.vector.quantize_mx(
+            out=hid_w[:].bitcast(FP8X4), scales=hid_s[:], in_=hid[:].rearrange("p s m t -> p (s m t)")
+        )
+        quant_cols(0)
+        second_product(0)
+        for s in range(PACK):
+            negate(s, 0)
+        sum_cols(1)
+        quant_cols(1)
+        second_product(1)
+
+        for s in range(PACK):
+            negate(s, 1)
+            means(s)
+        for s in range(PACK):
+            spread(s)
+        for s in range(PACK):
+            gather("vector" if s < 3 else "scalar", ng[0][:, s, :], neg[:, s, :], half_of(pair_t, 0))
+            finish(s, 0)
+        for s in range(PACK):
+            gather("scalar", ng[1][:, s, :], neg[:, s, :], half_of(pair_t, 1))
+        hand_on(0)
+        for s in range(PACK):
+            finish(s, 1)
+        hand_on(1)
+        for q in range(4):
+            queue = nc.scalar if q % 2 else nc.sync
+            queue.dma_start(out_2[0, 4 * q : 4 * q + 4, :].bitcast(I32), res_s[32 * q : 32 * q + 4, :].bitcast(I32))

@@ -1,6 +1,7 @@
 from contextlib import ExitStack
 
 import concourse.mybir as mybir
+from concourse.masks import make_identity
 
 K, T, S, H = 512, 2048, 512, 512
 FLOPS = 3 * 2 * 512 * 512 * 512
@@ -19,8 +20,12 @@ ALU = mybir.AluOpType
 
 P = 128
 PACK = 4
+RUN = 8
+VECTOR_WINDOW = 704
+SCALAR_WINDOW = 1024
 HALF = S // 2
 LIST_COLS = S // 16
+EARLY_COLS = 2 * S
 
 
 def tile_picked_ycoclus_max_po_kernel(
@@ -37,10 +42,6 @@ def tile_picked_ycoclus_max_po_kernel(
             nc.sync.dma_start(tile[:], src)
             return tile
 
-        def load_scale_rows(queue, plane, src):
-            for q in range(4):
-                queue.dma_start(plane[32 * q : 32 * q + 4, :].bitcast(I32), src[0, 4 * q : 4 * q + 4, :].bitcast(I32))
-
         def fill_scale_rows(queue, plane, src):
             for q in range(4):
                 rows = src[0, 4 * q : 4 * q + 4, :].bitcast(I32)
@@ -50,61 +51,63 @@ def tile_picked_ycoclus_max_po_kernel(
                 )
 
         x_plane = keep.tile([P, T], U8, name="x_plane", align_bytes=64)
-        e_plane = keep.tile([P, T], U8, name="e_plane", tag="e_plane", align_bytes=64)
-        w1_plane = keep.tile([P, H], U8, name="w1_plane", align_bytes=64)
+        e_plane = keep.tile([P, T], U8, name="e_plane", align_bytes=64)
+        w1_plane = keep.tile([P, H], U8, name="w1_plane", tag="w1_plane", align_bytes=64)
         w2_plane = keep.tile([P, H], U8, name="w2_plane", align_bytes=64)
-        nc.gpsimd.memset(e_plane[:].bitcast(I32), 0)
 
-        x_table = keep.tile([P, T], U32, name="x_table", tag="x_table", align_bytes=64)
+        x_table = keep.tile([P, T], U32, name="x_table", align_bytes=64)
         e_table = keep.tile([P, T], U32, name="e_table", align_bytes=64)
         w1_raw = keep.tile([P, 2 * H], U8, name="w1_raw", align_bytes=64)
         w2_raw = keep.tile([P, 2 * H], U8, name="w2_raw", align_bytes=64)
-        u1 = keep.tile([P, PACK], F32, name="u1")
-        u2 = keep.tile([P, PACK], F32, name="u2")
+        unit_rows = keep.tile([P, P], F32, name="unit_rows", align_bytes=64)
+        identity = keep.tile([P, P], F32, name="identity", align_bytes=64)
+        y = keep.tile([P, (PACK + 1) * S], F32, name="y", align_bytes=64)
+
+        nc.gpsimd.memset(unit_rows[:], 0.0)
+        nc.vector.memset(y[:, PACK * S :], 0.0)
+
+        def load_unit(first_row, src):
+            nc.gpsimd.dma_start(
+                unit_rows[first_row : first_row + PACK, :].rearrange("t (g r) -> t g r", r=RUN),
+                src.rearrange("(g t r) o -> t g (r o)", t=PACK, r=RUN),
+            )
+
+        make_identity(nc, identity[:])
+        load_unit(0, unit)
+        load_unit(PACK, unit2)
 
         fill_scale_rows(nc.sync, x_plane, x_scales)
         offs_t = load_list("offs_t", offs)
         nc.sync.dma_start(w1_raw[:].bitcast(I32), w1_words[0].bitcast(I32))
         nc.sync.dma_start(x_table[:].bitcast(I32), x_words[0].rearrange("p n t -> p (n t)").bitcast(I32))
         fill_scale_rows(nc.sync, w1_plane, w1_scales)
-        nc.sync.dma_start(u1[:], unit.rearrange("(p t) o -> p (t o)", t=PACK))
         col_t = load_list("col_t", col_)
         nc.sync.dma_start(e_table[:].bitcast(I32), e_words[0].rearrange("p n t -> p (n t)").bitcast(I32))
-        load_scale_rows(nc.gpsimd, e_plane, e_scales)
+        gr_t = load_list("gr_t", gr)
+        fill_scale_rows(nc.sync, e_plane, e_scales)
         nc.sync.dma_start(w2_raw[:].bitcast(I32), w2_words[0].bitcast(I32))
         fill_scale_rows(nc.sync, w2_plane, w2_scales)
-        gr_t = load_list("gr_t", gr)
-        nc.sync.dma_start(u2[:], unit2.rearrange("(p t) o -> p (t o)", t=PACK))
         gc_t = load_list("gc_t", gc)
         pair_t = load_list("pair_t", pair)
 
-        half_u1 = keep.tile([P, PACK], F32, name="half_u1")
-        half_u2 = keep.tile([P, PACK], F32, name="half_u2", tag="half_u2", align_bytes=64)
-        nc.scalar.activation(half_u1[:], u1[:], ACT.Copy, scale=0.5)
-        nc.scalar.activation(half_u2[:], u2[:], ACT.Copy, scale=0.5)
+        banks = [psum.tile([P, S], F32, name="bank%d" % b) for b in range(8)]
 
-        def deal_words(name, raw):
-            words = keep.tile([P, 2 * H], U8, name=name + "_words", align_bytes=64)
-            nc.vector.tensor_copy(
-                words[:].rearrange("p (t m b) -> p m t b", t=PACK, b=2),
-                raw[:].rearrange("p (m t b) -> p m t b", t=PACK, b=2),
-            )
-            return words
+        factors = keep.tile([P, 2 * PACK], F32, name="factors", tag="factors", align_bytes=64)
+        nc.tensor.transpose(banks[0][:, :P], unit_rows[:], identity[:])
+        nc.scalar.activation(factors[:], banks[0][:, : 2 * PACK], ACT.Copy, scale=0.5)
 
-        def deal_scales(name, plane):
-            scales = keep.tile([P, H], U8, name=name + "_scales", align_bytes=64)
+        def deal(name, raw, tag):
+            dealt = keep.tile(list(raw.shape), U8, name=name, tag=tag, align_bytes=64)
             nc.vector.tensor_copy(
-                scales[:].rearrange("p (t m) -> p m t", t=PACK),
-                plane[:].rearrange("p (m t) -> p m t", t=PACK),
+                dealt[:].bitcast(I32).rearrange("p (t g w) -> p t g w", t=PACK, g=P // RUN),
+                raw[:].bitcast(I32).rearrange("p (g t w) -> p t g w", t=PACK, g=P // RUN),
             )
-            return scales
+            return dealt
 
         def pick(name, dtype, table, entries, tag):
             picked = keep.tile([P, S], dtype, name=name, tag=tag, align_bytes=64)
             nc.vector.tensor_copy(picked[:], table[:].indirect(entries[:]))
             return picked
-
-        banks = [psum.tile([P, S], F32, name="bank%d" % b) for b in range(8)]
 
         def first_product(bank4, w_words, w_scales, words, scales):
             for t in range(PACK):
@@ -119,14 +122,14 @@ def tile_picked_ycoclus_max_po_kernel(
                 )
 
         x_sc = pick("x_sc", U8, x_plane, offs_t, "x_sc")
-        w1_w = deal_words("w1", w1_raw)
+        w1_w = deal("w1_w", w1_raw, "w1_w")
         x_w = pick("x_w", U32, x_table, offs_t, "x_w")
-        w1_s = deal_scales("w1", w1_plane)
+        w1_s = deal("w1_s", w1_plane, "w1_s")
         first_product(banks[:4], w1_w, w1_s, x_w, x_sc)
-        e_sc = pick("e_sc", U8, e_plane, col_t, "x_table")
-        e_w = pick("e_w", U32, e_table, col_t, "e_plane")
-        w2_w = deal_words("w2", w2_raw)
-        w2_s = deal_scales("w2", w2_plane)
+        e_w = pick("e_w", U32, e_table, col_t, "e_w")
+        w2_w = deal("w2_w", w2_raw, "w2_w")
+        w2_s = deal("w2_s", w2_plane, "w1_plane")
+        e_sc = pick("e_sc", U8, e_plane, col_t, "e_sc")
         first_product(banks[4:], w2_w, w2_s, e_w, e_sc)
 
         def half_of(entries, h):
@@ -138,23 +141,21 @@ def tile_picked_ycoclus_max_po_kernel(
             else:
                 nc.vector.tensor_copy(dst, window.indirect(entries))
 
-        y = keep.tile([P, PACK, S], F32, name="y", align_bytes=64)
         ye = keep.tile([P, PACK, S], F32, name="ye", align_bytes=64)
-        yg = [keep.tile([P, PACK, HALF], F32, name="yg%d" % h, align_bytes=64) for h in range(2)]
+        yg = keep.tile([P, PACK, S], F32, name="yg", align_bytes=64)
         eg = [keep.tile([P, PACK, HALF], F32, name="eg%d" % h, align_bytes=64) for h in range(2)]
-        hid = keep.tile([P, PACK, P, PACK], BF16, name="hid", tag="half_u2", align_bytes=64)
+        hid = keep.tile([P, PACK, P, PACK], BF16, name="hid", tag="factors", align_bytes=64)
         hid2 = [keep.tile([P, HALF, PACK], BF16, name="hid2_%d" % h, align_bytes=64) for h in range(2)]
         hid_w = keep.tile([P, S], U32, name="hid_w", align_bytes=64)
         hid_s = keep.tile([P, S], U8, name="hid_s", align_bytes=64)
         hid2_w = [keep.tile([P, HALF], U32, name="hid2_w%d" % h, align_bytes=64) for h in range(2)]
         hid2_s = [keep.tile([P, HALF], U8, name="hid2_s%d" % h, align_bytes=64) for h in range(2)]
 
-        def sum_rows(h):
-            m = slice(h * P // 2, (h + 1) * P // 2)
+        def sum_rows():
             nc.vector.tensor_tensor(
-                hid[:, :, m, :].rearrange("p s m t -> p m t s"),
-                yg[h][:].rearrange("p t (m s) -> p m t s", s=PACK),
-                y[:, :, h * HALF : (h + 1) * HALF].rearrange("p t (m s) -> p m t s", s=PACK),
+                hid[:].rearrange("p s m t -> p m t s"),
+                yg[:].rearrange("p t (m s) -> p m t s", s=PACK),
+                y[:, : PACK * S].rearrange("p (t m s) -> p m t s", t=PACK, s=PACK),
                 ALU.add,
             )
 
@@ -183,68 +184,74 @@ def tile_picked_ycoclus_max_po_kernel(
                     stop=True,
                 )
 
-        neg = keep.tile([P, PACK, S], F32, name="neg", align_bytes=64)
-        dev = keep.tile([P, S], F32, name="dev", align_bytes=64)
+        neg = keep.tile([P, PACK * S], F32, name="neg", align_bytes=64)
+        dev = keep.tile([P, S], F32, name="dev", tag="dev", align_bytes=64)
         neg_sum = [[keep.tile([P, 1], F32, name="neg_sum%d_%d" % (s, h)) for h in range(2)] for s in range(PACK)]
         dev_sum = [keep.tile([P, 1], F32, name="dev_sum%d" % s) for s in range(PACK)]
         two_mu = [keep.tile([P, 1], F32, name="two_mu%d" % s) for s in range(PACK)]
         neg_mu = [keep.tile([P, 1], F32, name="neg_mu%d" % s) for s in range(PACK)]
         den = [keep.tile([P, 1], F32, name="den%d" % s) for s in range(PACK)]
         inv = [keep.tile([P, 1], F32, name="inv%d" % s) for s in range(PACK)]
-        ng = [keep.tile([P, PACK, HALF], F32, name="ng%d" % h, align_bytes=64) for h in range(2)]
-        top = [keep.tile([P, PACK, HALF], F32, name="top%d" % h, align_bytes=64) for h in range(2)]
-        res = [keep.tile([P, PACK, HALF], F32, name="res%d" % h, align_bytes=64) for h in range(2)]
-        res_b = [keep.tile([P, HALF, PACK], BF16, name="res_b%d" % h, align_bytes=64) for h in range(2)]
-        res_w = [keep.tile([P, HALF], U32, name="res_w%d" % h, align_bytes=64) for h in range(2)]
+        early = keep.tile([P, EARLY_COLS], F32, name="early", align_bytes=64)
+        top = keep.tile([P, PACK, S], F32, name="top", align_bytes=64)
+        res = keep.tile([P, PACK, S], F32, name="res", align_bytes=64)
+        res_b = keep.tile([P, S, PACK], BF16, name="res_b", align_bytes=64)
+        res_w = keep.tile([P, S], U32, name="res_w", align_bytes=64)
         res_s = keep.tile([P, S], U8, name="res_s", align_bytes=64)
         out_rows = out_0.rearrange("(p s) e -> p s e", s=PACK)
         out_words = out_1[0].rearrange("p e t -> p (e t)").bitcast(I32)
 
         def negate(s, h):
             cols = slice(h * HALF, (h + 1) * HALF)
-            nc.scalar.activation(neg[:, s, cols], banks[s][:, cols], ACT.Copy, scale=-1.0, accum_out=neg_sum[s][h][:])
+            nc.scalar.activation(
+                neg[:, s * S + cols.start : s * S + cols.stop], banks[s][:, cols], ACT.Copy, scale=-1.0,
+                accum_out=neg_sum[s][h][:],
+            )
 
         def means(s):
-            nc.gpsimd.tensor_scalar(neg_mu[s][:], neg_sum[s][0][:], neg_sum[s][1][:], 1.0 / S, ALU.add, ALU.mult)
             nc.gpsimd.tensor_scalar(two_mu[s][:], neg_sum[s][0][:], neg_sum[s][1][:], -2.0 / S, ALU.add, ALU.mult)
+            nc.gpsimd.tensor_scalar(neg_mu[s][:], neg_sum[s][0][:], neg_sum[s][1][:], 1.0 / S, ALU.add, ALU.mult)
 
         def spread(s):
-            nc.scalar.activation(dev[:], banks[s][:], ACT.Abs, bias=neg_mu[s][:], accum_out=dev_sum[s][:])
-            nc.gpsimd.tensor_scalar(den[s][:], dev_sum[s][:], 1.0 / S, 0.2, ALU.mult, ALU.add)
-
-        def finish(s, h):
-            cols = slice(h * HALF, (h + 1) * HALF)
-            nc.vector.scalar_tensor_tensor(
-                top[h][:, s, :], ng[h][:, s, :], two_mu[s][:], banks[s][:, cols], ALU.add, ALU.max
+            nc.scalar.activation(
+                dev[:], neg[:, s * S : (s + 1) * S], ACT.Abs, scale=2.0, bias=two_mu[s][:], accum_out=dev_sum[s][:]
             )
-            if h == 0:
-                nc.vector.reciprocal(inv[s][:], den[s][:])
-            nc.vector.tensor_scalar(res[h][:, s, :], top[h][:, s, :], neg_mu[s][:], inv[s][:], ALU.add, ALU.mult)
-            nc.sync.dma_start(out_rows[:, s, cols], res[h][:, s, :])
+            nc.gpsimd.tensor_scalar(den[s][:], dev_sum[s][:], 0.5 / S, 0.2, ALU.mult, ALU.add)
 
-        def hand_on(h):
-            cols = slice(h * HALF, (h + 1) * HALF)
+        def larger(s, cols, picked):
+            nc.vector.scalar_tensor_tensor(top[:, s, cols], picked, two_mu[s][:], banks[s][:, cols], ALU.add, ALU.max)
+
+        def finish(s, cols):
+            nc.vector.tensor_scalar(res[:, s, cols], top[:, s, cols], neg_mu[s][:], inv[s][:], ALU.add, ALU.mult)
+            nc.sync.dma_start(out_rows[:, s, cols], res[:, s, cols])
+
+        def round_cols(cols):
             nc.vector.tensor_copy(
-                res_b[h][:].rearrange("p (c i) t -> p c t i", i=4),
-                res[h][:].rearrange("p t (c i) -> p c t i", i=4),
+                res_b[:, cols, :].rearrange("p (c i) t -> p c t i", i=4),
+                res[:, :, cols].rearrange("p t (c i) -> p c t i", i=4),
             )
+
+        def quant_out(cols):
             nc.vector.quantize_mx(
-                out=res_w[h][:].bitcast(FP8X4), scales=res_s[:, cols], in_=res_b[h][:].rearrange("p e t -> p (e t)")
+                out=res_w[:, cols].bitcast(FP8X4),
+                scales=res_s[:, cols],
+                in_=res_b[:, cols, :].rearrange("p e t -> p (e t)"),
             )
-            nc.sync.dma_start(out_words[:, cols], res_w[h][:].bitcast(I32))
+
+        def store_words(cols):
+            nc.sync.dma_start(out_words[:, cols], res_w[:, cols].bitcast(I32))
 
         for t in range(PACK):
-            nc.scalar.activation(y[:, t, :], banks[t][:], ACT.Copy, scale=half_u1[:, t : t + 1])
+            nc.scalar.activation(y[:, t * S : (t + 1) * S], banks[t][:], ACT.Copy, scale=factors[:, t : t + 1])
         for t in range(PACK):
-            gather("scalar", yg[0][:, t, :], y[:, t, :], half_of(gr_t, 0))
+            gather("scalar", yg[:, t, :], y[:, t * S : t * S + SCALAR_WINDOW], gr_t[:])
         for t in range(PACK):
-            nc.vector.tensor_scalar(ye[:, t, :], banks[4 + t][:], half_u2[:, t : t + 1], None, ALU.mult)
+            nc.vector.tensor_scalar(
+                ye[:, t, :], banks[PACK + t][:], factors[:, PACK + t : PACK + t + 1], None, ALU.mult
+            )
         for t in range(PACK):
-            gather("scalar", yg[1][:, t, :], y[:, t, :], half_of(gr_t, 1))
-        sum_rows(0)
-        for t in range(PACK):
-            gather("vector" if t < 1 else "scalar", eg[0][:, t, :], ye[:, t, :], half_of(gc_t, 0))
-        sum_rows(1)
+            gather("vector" if t < 2 else "scalar", eg[0][:, t, :], ye[:, t, :], half_of(gc_t, 0))
+        sum_rows()
         for t in range(PACK):
             gather("scalar", eg[1][:, t, :], ye[:, t, :], half_of(gc_t, 1))
         sum_cols(0)
@@ -264,15 +271,35 @@ def tile_picked_ycoclus_max_po_kernel(
             means(s)
         for s in range(PACK):
             spread(s)
-        for s in range(PACK):
-            gather("vector" if s < 3 else "scalar", ng[0][:, s, :], neg[:, s, :], half_of(pair_t, 0))
-            finish(s, 0)
-        for s in range(PACK):
-            gather("scalar", ng[1][:, s, :], neg[:, s, :], half_of(pair_t, 1))
-        hand_on(0)
-        for s in range(PACK):
-            finish(s, 1)
-        hand_on(1)
+        late = keep.tile([P, PACK * S - EARLY_COLS], F32, name="late", tag="dev", align_bytes=64)
+
+        def paired(s, cols):
+            lo, hi = s * S + cols.start, s * S + cols.stop
+            return early[:, lo:hi] if hi <= EARLY_COLS else late[:, lo - EARLY_COLS : hi - EARLY_COLS]
+
+        halves = [slice(0, HALF), slice(HALF, S)]
+        for s in range(2):
+            gather("vector", paired(s, slice(0, S)), neg[:, s * S : s * S + VECTOR_WINDOW], pair_t[:])
+        gather("scalar", paired(2, slice(0, S)), neg[:, 2 * S : 2 * S + SCALAR_WINDOW], pair_t[:])
+        for h in range(2):
+            gather("scalar", paired(3, halves[h]), neg[:, 3 * S :], half_of(pair_t, h))
+        steps = [(s, slice(0, S)) for s in range(PACK - 1)] + [(PACK - 1, cols) for cols in halves]
+        for n, (s, cols) in enumerate(steps):
+            larger(s, cols, paired(s, cols))
+            if cols.start == 0:
+                nc.vector.reciprocal(inv[s][:], den[s][:])
+            if n > 0:
+                finish(*steps[n - 1])
+        round_cols(halves[0])
+        finish(*steps[-1])
+        quant_out(halves[0])
+        store_words(halves[0])
+        parts = [slice(HALF, HALF + HALF // 2), slice(HALF + HALF // 2, S)]
+        for part in parts:
+            round_cols(part)
+        for part in parts:
+            quant_out(part)
+        store_words(halves[1])
         for q in range(4):
             queue = nc.scalar if q % 2 else nc.sync
             queue.dma_start(out_2[0, 4 * q : 4 * q + 4, :].bitcast(I32), res_s[32 * q : 32 * q + 4, :].bitcast(I32))

@@ -59,42 +59,37 @@ def tile_picked_ycoclus_max_po_kernel(
         e_table = keep.tile([P, T], U32, name="e_table", align_bytes=64)
         w1_raw = keep.tile([P, 2 * H], U8, name="w1_raw", align_bytes=64)
         w2_raw = keep.tile([P, 2 * H], U8, name="w2_raw", align_bytes=64)
-        unit_rows = keep.tile([P, P], F32, name="unit_rows", align_bytes=64)
+        unit_blocks = keep.tile([P, 2, PACK * RUN], F32, name="unit_blocks", align_bytes=64)
         identity = keep.tile([P, P], F32, name="identity", align_bytes=64)
-        y = keep.tile([P, (PACK + 1) * S], F32, name="y", align_bytes=64)
+        y = keep.tile([P, PACK, S], F32, name="y", align_bytes=64)
 
-        nc.gpsimd.memset(unit_rows[:], 0.0)
-        nc.vector.memset(y[:, PACK * S :], 0.0)
-
-        def load_unit(first_row, src):
-            nc.gpsimd.dma_start(
-                unit_rows[first_row : first_row + PACK, :].rearrange("t (g r) -> t g r", r=RUN),
-                src.rearrange("(g t r) o -> t g (r o)", t=PACK, r=RUN),
-            )
+        def load_unit(which, src):
+            blocks = src.rearrange("(g c) o -> g (c o)", c=PACK * RUN)
+            nc.sync.dma_start(unit_blocks[:, which, :], blocks.unsqueeze(1).to_broadcast([P // RUN, RUN, PACK * RUN]))
 
         make_identity(nc, identity[:])
-        load_unit(0, unit)
-        load_unit(PACK, unit2)
+        own_place = keep.tile([P, RUN], F32, name="own_place")
+        nc.vector.tensor_reduce(
+            own_place[:], identity[:].rearrange("p (g r) -> p r g", r=RUN), mybir.AxisListType.X, ALU.add
+        )
 
         fill_scale_rows(nc.sync, x_plane, x_scales)
         offs_t = load_list("offs_t", offs)
         nc.sync.dma_start(w1_raw[:].bitcast(I32), w1_words[0].bitcast(I32))
         nc.sync.dma_start(x_table[:].bitcast(I32), x_words[0].rearrange("p n t -> p (n t)").bitcast(I32))
         fill_scale_rows(nc.sync, w1_plane, w1_scales)
-        col_t = load_list("col_t", col_)
+        load_unit(0, unit)
+        load_unit(1, unit2)
         nc.sync.dma_start(e_table[:].bitcast(I32), e_words[0].rearrange("p n t -> p (n t)").bitcast(I32))
-        gr_t = load_list("gr_t", gr)
+        col_t = load_list("col_t", col_)
         fill_scale_rows(nc.sync, e_plane, e_scales)
+        gr_t = load_list("gr_t", gr)
         nc.sync.dma_start(w2_raw[:].bitcast(I32), w2_words[0].bitcast(I32))
         fill_scale_rows(nc.sync, w2_plane, w2_scales)
         gc_t = load_list("gc_t", gc)
         pair_t = load_list("pair_t", pair)
 
         banks = [psum.tile([P, S], F32, name="bank%d" % b) for b in range(8)]
-
-        factors = keep.tile([P, 2 * PACK], F32, name="factors", tag="factors", align_bytes=64)
-        nc.tensor.transpose(banks[0][:, :P], unit_rows[:], identity[:])
-        nc.scalar.activation(factors[:], banks[0][:, : 2 * PACK], ACT.Copy, scale=0.5)
 
         def deal(name, raw, tag):
             dealt = keep.tile(list(raw.shape), U8, name=name, tag=tag, align_bytes=64)
@@ -126,6 +121,17 @@ def tile_picked_ycoclus_max_po_kernel(
         x_w = pick("x_w", U32, x_table, offs_t, "x_w")
         w1_s = deal("w1_s", w1_plane, "w1_s")
         first_product(banks[:4], w1_w, w1_s, x_w, x_sc)
+        masked = keep.tile([P, 2 * PACK, RUN], F32, name="masked")
+        nc.vector.scalar_tensor_tensor(
+            masked[:],
+            unit_blocks[:].rearrange("p u (t r) -> p (u t) r", r=RUN),
+            0.5,
+            own_place[:].unsqueeze(1).to_broadcast([P, 2 * PACK, RUN]),
+            ALU.mult,
+            ALU.mult,
+        )
+        factors = keep.tile([P, 2 * PACK], F32, name="factors", tag="factors", align_bytes=64)
+        nc.vector.tensor_reduce(factors[:], masked[:], mybir.AxisListType.X, ALU.add)
         e_w = pick("e_w", U32, e_table, col_t, "e_w")
         w2_w = deal("w2_w", w2_raw, "w2_w")
         w2_s = deal("w2_s", w2_plane, "w1_plane")
@@ -142,7 +148,7 @@ def tile_picked_ycoclus_max_po_kernel(
                 nc.vector.tensor_copy(dst, window.indirect(entries))
 
         ye = keep.tile([P, PACK, S], F32, name="ye", align_bytes=64)
-        yg = keep.tile([P, PACK, S], F32, name="yg", align_bytes=64)
+        yg = [keep.tile([P, PACK, HALF], F32, name="yg%d" % h, align_bytes=64) for h in range(2)]
         eg = [keep.tile([P, PACK, HALF], F32, name="eg%d" % h, align_bytes=64) for h in range(2)]
         hid = keep.tile([P, PACK, P, PACK], BF16, name="hid", tag="factors", align_bytes=64)
         hid2 = [keep.tile([P, HALF, PACK], BF16, name="hid2_%d" % h, align_bytes=64) for h in range(2)]
@@ -151,11 +157,12 @@ def tile_picked_ycoclus_max_po_kernel(
         hid2_w = [keep.tile([P, HALF], U32, name="hid2_w%d" % h, align_bytes=64) for h in range(2)]
         hid2_s = [keep.tile([P, HALF], U8, name="hid2_s%d" % h, align_bytes=64) for h in range(2)]
 
-        def sum_rows():
+        def sum_rows(h):
+            m = slice(h * P // 2, (h + 1) * P // 2)
             nc.vector.tensor_tensor(
-                hid[:].rearrange("p s m t -> p m t s"),
-                yg[:].rearrange("p t (m s) -> p m t s", s=PACK),
-                y[:, : PACK * S].rearrange("p (t m s) -> p m t s", t=PACK, s=PACK),
+                hid[:, :, m, :].rearrange("p s m t -> p m t s"),
+                yg[h][:].rearrange("p t (m s) -> p m t s", s=PACK),
+                y[:, :, h * HALF : (h + 1) * HALF].rearrange("p t (m s) -> p m t s", s=PACK),
                 ALU.add,
             )
 
@@ -242,16 +249,18 @@ def tile_picked_ycoclus_max_po_kernel(
             nc.sync.dma_start(out_words[:, cols], res_w[:, cols].bitcast(I32))
 
         for t in range(PACK):
-            nc.scalar.activation(y[:, t * S : (t + 1) * S], banks[t][:], ACT.Copy, scale=factors[:, t : t + 1])
-        for t in range(PACK):
-            gather("scalar", yg[:, t, :], y[:, t * S : t * S + SCALAR_WINDOW], gr_t[:])
+            nc.scalar.activation(y[:, t, :], banks[t][:], ACT.Copy, scale=factors[:, t : t + 1])
+        for h in range(2):
+            for t in range(PACK):
+                gather("scalar", yg[h][:, t, :], y[:, t, :], half_of(gr_t, h))
         for t in range(PACK):
             nc.vector.tensor_scalar(
                 ye[:, t, :], banks[PACK + t][:], factors[:, PACK + t : PACK + t + 1], None, ALU.mult
             )
+        sum_rows(0)
         for t in range(PACK):
-            gather("vector" if t < 2 else "scalar", eg[0][:, t, :], ye[:, t, :], half_of(gc_t, 0))
-        sum_rows()
+            gather("vector" if t < 3 else "scalar", eg[0][:, t, :], ye[:, t, :], half_of(gc_t, 0))
+        sum_rows(1)
         for t in range(PACK):
             gather("scalar", eg[1][:, t, :], ye[:, t, :], half_of(gc_t, 1))
         sum_cols(0)

@@ -72,6 +72,8 @@ def tile_picked_ycoclus_max_po_kernel(
         nc.vector.tensor_reduce(
             own_place[:], identity[:].rearrange("p (g r) -> p r g", r=RUN), mybir.AxisListType.X, ALU.add
         )
+        half_place = keep.tile([P, RUN], F32, name="half_place")
+        nc.scalar.activation(half_place[:], own_place[:], ACT.Copy, scale=0.5)
 
         fill_scale_rows(nc.sync, x_plane, x_scales)
         offs_t = load_list("offs_t", offs)
@@ -122,12 +124,10 @@ def tile_picked_ycoclus_max_po_kernel(
         w1_s = deal("w1_s", w1_plane, "w1_s")
         first_product(banks[:4], w1_w, w1_s, x_w, x_sc)
         masked = keep.tile([P, 2 * PACK, RUN], F32, name="masked")
-        nc.vector.scalar_tensor_tensor(
+        nc.vector.tensor_tensor(
             masked[:],
             unit_blocks[:].rearrange("p u (t r) -> p (u t) r", r=RUN),
-            0.5,
-            own_place[:].unsqueeze(1).to_broadcast([P, 2 * PACK, RUN]),
-            ALU.mult,
+            half_place[:].unsqueeze(1).to_broadcast([P, 2 * PACK, RUN]),
             ALU.mult,
         )
         factors = keep.tile([P, 2 * PACK], F32, name="factors", tag="factors", align_bytes=64)
@@ -202,7 +202,7 @@ def tile_picked_ycoclus_max_po_kernel(
         early = keep.tile([P, EARLY_COLS], F32, name="early", align_bytes=64)
         top = keep.tile([P, PACK, S], F32, name="top", align_bytes=64)
         res = keep.tile([P, PACK, S], F32, name="res", align_bytes=64)
-        res_b = keep.tile([P, S, PACK], BF16, name="res_b", align_bytes=64)
+        res_b = [keep.tile([P, HALF, PACK], BF16, name="res_b%d" % h, align_bytes=64) for h in range(2)]
         res_w = keep.tile([P, S], U32, name="res_w", align_bytes=64)
         res_s = keep.tile([P, S], U8, name="res_s", align_bytes=64)
         out_rows = out_0.rearrange("(p s) e -> p s e", s=PACK)
@@ -232,9 +232,13 @@ def tile_picked_ycoclus_max_po_kernel(
             nc.vector.tensor_scalar(res[:, s, cols], top[:, s, cols], neg_mu[s][:], inv[s][:], ALU.add, ALU.mult)
             nc.sync.dma_start(out_rows[:, s, cols], res[:, s, cols])
 
-        def round_cols(cols):
-            nc.vector.tensor_copy(
-                res_b[:, cols, :].rearrange("p (c i) t -> p c t i", i=4),
+        def rounded(cols):
+            h = cols.start // HALF
+            return res_b[h][:, cols.start - h * HALF : cols.stop - h * HALF, :]
+
+        def round_cols(copy, cols):
+            copy(
+                rounded(cols).rearrange("p (c i) t -> p c t i", i=4),
                 res[:, :, cols].rearrange("p t (c i) -> p c t i", i=4),
             )
 
@@ -242,7 +246,7 @@ def tile_picked_ycoclus_max_po_kernel(
             nc.vector.quantize_mx(
                 out=res_w[:, cols].bitcast(FP8X4),
                 scales=res_s[:, cols],
-                in_=res_b[:, cols, :].rearrange("p e t -> p (e t)"),
+                in_=rounded(cols).rearrange("p e t -> p (e t)"),
             )
 
         def store_words(cols):
@@ -299,16 +303,16 @@ def tile_picked_ycoclus_max_po_kernel(
                 nc.vector.reciprocal(inv[s][:], den[s][:])
             if n > 0:
                 finish(*steps[n - 1])
-        round_cols(halves[0])
+        round_cols(nc.scalar.copy, halves[0])
         finish(*steps[-1])
-        quant_out(halves[0])
-        store_words(halves[0])
         parts = [slice(HALF, HALF + HALF // 2), slice(HALF + HALF // 2, S)]
         for part in parts:
-            round_cols(part)
+            round_cols(nc.vector.tensor_copy, part)
         for part in parts:
             quant_out(part)
         store_words(halves[1])
+        quant_out(halves[0])
+        store_words(halves[0])
         for q in range(4):
             queue = nc.scalar if q % 2 else nc.sync
             queue.dma_start(out_2[0, 4 * q : 4 * q + 4, :].bitcast(I32), res_s[32 * q : 32 * q + 4, :].bitcast(I32))

from contextlib import ExitStack

import concourse.mybir as mybir
from concourse.masks import make_identity

K, T, S, H = 512, 2048, 512, 512
FLOPS = 3 * 2 * 512 * 512 * 512
BYTES = 2 * (S * 512 + S * 16) + 2 * (128 * 1024 + 16 * 512) + 2 * 2048 + 5 * 4096 + 512 * 512 * 4 + 512 * 512 + 16 * 512

F32 = mybir.dt.float32
BF16 = mybir.dt.bfloat16
I32 = mybir.dt.int32
U32 = mybir.dt.uint32
U16 = mybir.dt.uint16
U8 = mybir.dt.uint8
FP8X4 = mybir.dt.float8_e4m3fn_x4
FP4X4 = mybir.dt.float4_e2m1fn_x4
ACT = mybir.ActivationFunctionType
ALU = mybir.AluOpType

P = 128
PACK = 4
RUN = 8
VECTOR_WINDOW = 704
SCALAR_WINDOW = 1024
HALF = S // 2
LIST_COLS = S // 16
EARLY_COLS = 2 * S


def tile_picked_ycoclus_max_po_kernel(
    tc, x_words, x_scales, w1_words, w1_scales, e_words, e_scales, w2_words, w2_scales,
    unit, unit2, offs, col_, gr, gc, pair, out_0, out_1, out_2,
):
    nc = tc.nc
    with ExitStack() as ctx:
        keep = ctx.enter_context(tc.tile_pool(name="keep", bufs=1))
        psum = ctx.enter_context(tc.psum_pool(name="psum", bufs=1))

        def load_list(name, src):
            tile = keep.tile([P, LIST_COLS], U16, name=name)
            nc.sync.dma_start(tile[:], src)
            return tile

        def fill_scale_rows(queue, plane, src):
            for q in range(4):
                rows = src[0, 4 * q : 4 * q + 4, :].bitcast(I32)
                queue.dma_start(
                    plane[32 * q : 32 * q + 32, :].bitcast(I32),
                    rows.unsqueeze(0).to_broadcast([8, 4, rows.shape[1]]),
                )

        x_plane = keep.tile([P, T], U8, name="x_plane", align_bytes=64)
        e_plane = keep.tile([P, T], U8, name="e_plane", align_bytes=64)
        w1_plane = keep.tile([P, H], U8, name="w1_plane", tag="w1_plane", align_bytes=64)
        w2_plane = keep.tile([P, H], U8, name="w2_plane", align_bytes=64)

        x_table = keep.tile([P, T], U32, name="x_table", align_bytes=64)
        e_table = keep.tile([P, T], U32, name="e_table", align_bytes=64)
        w1_raw = keep.tile([P, 2 * H], U8, name="w1_raw", align_bytes=64)
        w2_raw = keep.tile([P, 2 * H], U8, name="w2_raw", align_bytes=64)
        unit_blocks = keep.tile([P, 2, PACK * RUN], F32, name="unit_blocks", align_bytes=64)
        identity = keep.tile([P, P], F32, name="identity", align_bytes=64)
        y = keep.tile([P, PACK, S], F32, name="y", align_bytes=64)

        def load_unit(which, src):
            blocks = src.rearrange("(g c) o -> g (c o)", c=PACK * RUN)
            nc.sync.dma_start(unit_blocks[:, which, :], blocks.unsqueeze(1).to_broadcast([P // RUN, RUN, PACK * RUN]))

        make_identity(nc, identity[:])
        own_place = keep.tile([P, RUN], F32, name="own_place")
        nc.vector.tensor_reduce(
            own_place[:], identity[:].rearrange("p (g r) -> p r g", r=RUN), mybir.AxisListType.X, ALU.add
        )
        half_place = keep.tile([P, RUN], F32, name="half_place")
        nc.scalar.activation(half_place[:], own_place[:], ACT.Copy, scale=0.5)

        fill_scale_rows(nc.sync, x_plane, x_scales)
        offs_t = load_list("offs_t", offs)
        nc.sync.dma_start(w1_raw[:].bitcast(I32), w1_words[0].bitcast(I32))
        nc.sync.dma_start(x_table[:].bitcast(I32), x_words[0].rearrange("p n t -> p (n t)").bitcast(I32))
        fill_scale_rows(nc.sync, w1_plane, w1_scales)
        load_unit(0, unit)
        load_unit(1, unit2)
        nc.sync.dma_start(e_table[:].bitcast(I32), e_words[0].rearrange("p n t -> p (n t)").bitcast(I32))
        col_t = load_list("col_t", col_)
        fill_scale_rows(nc.sync, e_plane, e_scales)
        gr_t = load_list("gr_t", gr)
        nc.sync.dma_start(w2_raw[:].bitcast(I32), w2_words[0].bitcast(I32))
        fill_scale_rows(nc.sync, w2_plane, w2_scales)
        gc_t = load_list("gc_t", gc)
        pair_t = load_list("pair_t", pair)

        banks = [psum.tile([P, S], F32, name="bank%d" % b) for b in range(8)]

        def deal(name, raw, tag):
            dealt = keep.tile(list(raw.shape), U8, name=name, tag=tag, align_bytes=64)
            nc.vector.tensor_copy(
                dealt[:].bitcast(I32).rearrange("p (t g w) -> p t g w", t=PACK, g=P // RUN),
                raw[:].bitcast(I32).rearrange("p (g t w) -> p t g w", t=PACK, g=P // RUN),
            )
            return dealt

        def pick(name, dtype, table, entries, tag):
            picked = keep.tile([P, S], dtype, name=name, tag=tag, align_bytes=64)
            nc.vector.tensor_copy(picked[:], table[:].indirect(entries[:]))
            return picked

        def first_product(bank4, w_words, w_scales, words, scales):
            for t in range(PACK):
                nc.tensor.matmul_mx(
                    out=bank4[t][:],
                    lhsT=w_words[:, 2 * P * t : 2 * P * (t + 1)].bitcast(FP4X4),
                    lhsT_scale=w_scales[:, P * t : P * (t + 1)],
                    rhs=words[:].bitcast(FP8X4),
                    rhs_scale=scales[:],
                    start=True,
                    stop=True,
                )

        x_sc = pick("x_sc", U8, x_plane, offs_t, "x_sc")
        w1_w = deal("w1_w", w1_raw, "w1_w")
        x_w = pick("x_w", U32, x_table, offs_t, "x_w")
        w1_s = deal("w1_s", w1_plane, "w1_s")
        first_product(banks[:4], w1_w, w1_s, x_w, x_sc)
        masked = keep.tile([P, 2 * PACK, RUN], F32, name="masked")
        nc.vector.tensor_tensor(
            masked[:],
            unit_blocks[:].rearrange("p u (t r) -> p (u t) r", r=RUN),
            half_place[:].unsqueeze(1).to_broadcast([P, 2 * PACK, RUN]),
            ALU.mult,
        )
        factors = keep.tile([P, 2 * PACK], F32, name="factors", tag="factors", align_bytes=64)
        nc.vector.tensor_reduce(factors[:], masked[:], mybir.AxisListType.X, ALU.add)
        e_w = pick("e_w", U32, e_table, col_t, "e_w")
        w2_w = deal("w2_w", w2_raw, "w2_w")
        w2_s = deal("w2_s", w2_plane, "w1_plane")
        e_sc = pick("e_sc", U8, e_plane, col_t, "e_sc")
        first_product(banks[4:], w2_w, w2_s, e_w, e_sc)

        def half_of(entries, h):
            return entries[:, h * LIST_COLS // 2 : (h + 1) * LIST_COLS // 2]

        def gather(engine, dst, window, entries):
            if engine == "scalar":
                nc.scalar.activation(dst, window.indirect(entries), ACT.Copy)
            else:
                nc.vector.tensor_copy(dst, window.indirect(entries))

        ye = keep.tile([P, PACK, S], F32, name="ye", align_bytes=64)
        yg = [keep.tile([P, PACK, HALF], F32, name="yg%d" % h, align_bytes=64) for h in range(2)]
        eg = [keep.tile([P, PACK, HALF], F32, name="eg%d" % h, align_bytes=64) for h in range(2)]
        hid = keep.tile([P, PACK, P, PACK], BF16, name="hid", tag="factors", align_bytes=64)
        hid2 = [keep.tile([P, HALF, PACK], BF16, name="hid2_%d" % h, align_bytes=64) for h in range(2)]
        hid_w = keep.tile([P, S], U32, name="hid_w", align_bytes=64)
        hid_s = keep.tile([P, S], U8, name="hid_s", align_bytes=64)
        hid2_w = [keep.tile([P, HALF], U32, name="hid2_w%d" % h, align_bytes=64) for h in range(2)]
        hid2_s = [keep.tile([P, HALF], U8, name="hid2_s%d" % h, align_bytes=64) for h in range(2)]

        def sum_rows(h):
            m = slice(h * P // 2, (h + 1) * P // 2)
            nc.vector.tensor_tensor(
                hid[:, :, m, :].rearrange("p s m t -> p m t s"),
                yg[h][:].rearrange("p t (m s) -> p m t s", s=PACK),
                y[:, :, h * HALF : (h + 1) * HALF].rearrange("p t (m s) -> p m t s", s=PACK),
                ALU.add,
            )

        def sum_cols(h):
            nc.vector.tensor_tensor(
                hid2[h][:].rearrange("p (c i) t -> p c t i", i=4),
                eg[h][:].rearrange("p t (c i) -> p c t i", i=4),
                ye[:, :, h * HALF : (h + 1) * HALF].rearrange("p t (c i) -> p c t i", i=4),
                ALU.add,
            )

        def quant_cols(h):
            nc.vector.quantize_mx(
                out=hid2_w[h][:].bitcast(FP8X4), scales=hid2_s[h][:], in_=hid2[h][:].rearrange("p e t -> p (e t)")
            )

        def second_product(h):
            for s in range(PACK):
                nc.tensor.matmul_mx(
                    out=banks[s][:, h * HALF : (h + 1) * HALF],
                    lhsT=hid_w[:, P * s : P * (s + 1)].bitcast(FP8X4),
                    lhsT_scale=hid_s[:, P * s : P * (s + 1)],
                    rhs=hid2_w[h][:].bitcast(FP8X4),
                    rhs_scale=hid2_s[h][:],
                    start=True,
                    stop=True,
                )

        neg = keep.tile([P, PACK * S], F32, name="neg", align_bytes=64)
        dev = keep.tile([P, S], F32, name="dev", tag="dev", align_bytes=64)
        neg_sum = [[keep.tile([P, 1], F32, name="neg_sum%d_%d" % (s, h)) for h in range(2)] for s in range(PACK)]
        dev_sum = [keep.tile([P, 1], F32, name="dev_sum%d" % s) for s in range(PACK)]
        two_mu = [keep.tile([P, 1], F32, name="two_mu%d" % s) for s in range(PACK)]
        neg_mu = [keep.tile([P, 1], F32, name="neg_mu%d" % s) for s in range(PACK)]
        den = [keep.tile([P, 1], F32, name="den%d" % s) for s in range(PACK)]
        inv = [keep.tile([P, 1], F32, name="inv%d" % s) for s in range(PACK)]
        early = keep.tile([P, EARLY_COLS], F32, name="early", align_bytes=64)
        top = keep.tile([P, PACK, S], F32, name="top", align_bytes=64)
        res = keep.tile([P, PACK, S], F32, name="res", align_bytes=64)
        res_b = [keep.tile([P, HALF, PACK], BF16, name="res_b%d" % h, align_bytes=64) for h in range(2)]
        res_w = keep.tile([P, S], U32, name="res_w", align_bytes=64)
        res_s = keep.tile([P, S], U8, name="res_s", align_bytes=64)
        out_rows = out_0.rearrange("(p s) e -> p s e", s=PACK)
        out_words = out_1[0].rearrange("p e t -> p (e t)").bitcast(I32)

        def negate(s, h):
            cols = slice(h * HALF, (h + 1) * HALF)
            nc.scalar.activation(
                neg[:, s * S + cols.start : s * S + cols.stop], banks[s][:, cols], ACT.Copy, scale=-1.0,
                accum_out=neg_sum[s][h][:],
            )

        def means(s):
            nc.gpsimd.tensor_scalar(two_mu[s][:], neg_sum[s][0][:], neg_sum[s][1][:], -2.0 / S, ALU.add, ALU.mult)
            nc.gpsimd.tensor_scalar(neg_mu[s][:], neg_sum[s][0][:], neg_sum[s][1][:], 1.0 / S, ALU.add, ALU.mult)

        def spread(s):
            nc.scalar.activation(
                dev[:], neg[:, s * S : (s + 1) * S], ACT.Abs, scale=2.0, bias=two_mu[s][:], accum_out=dev_sum[s][:]
            )
            nc.gpsimd.tensor_scalar(den[s][:], dev_sum[s][:], 0.5 / S, 0.2, ALU.mult, ALU.add)

        def larger(s, cols, picked):
            nc.vector.scalar_tensor_tensor(top[:, s, cols], picked, two_mu[s][:], banks[s][:, cols], ALU.add, ALU.max)

        def finish(s, cols):
            nc.vector.tensor_scalar(res[:, s, cols], top[:, s, cols], neg_mu[s][:], inv[s][:], ALU.add, ALU.mult)
            nc.sync.dma_start(out_rows[:, s, cols], res[:, s, cols])

        def rounded(cols):
            h = cols.start // HALF
            return res_b[h][:, cols.start - h * HALF : cols.stop - h * HALF, :]

        def round_cols(copy, cols):
            copy(
                rounded(cols).rearrange("p (c i) t -> p c t i", i=4),
                res[:, :, cols].rearrange("p t (c i) -> p c t i", i=4),
            )

        def quant_out(cols):
            nc.vector.quantize_mx(
                out=res_w[:, cols].bitcast(FP8X4),
                scales=res_s[:, cols],
                in_=rounded(cols).rearrange("p e t -> p (e t)"),
            )

        def store_words(cols):
            nc.sync.dma_start(out_words[:, cols], res_w[:, cols].bitcast(I32))

        for t in range(PACK):
            nc.scalar.activation(y[:, t, :], banks[t][:], ACT.Copy, scale=factors[:, t : t + 1])
        for h in range(2):
            for t in range(PACK):
                gather("scalar", yg[h][:, t, :], y[:, t, :], half_of(gr_t, h))
        for t in range(PACK):
            nc.vector.tensor_scalar(
                ye[:, t, :], banks[PACK + t][:], factors[:, PACK + t : PACK + t + 1], None, ALU.mult
            )
        sum_rows(0)
        for t in range(PACK):
            gather("vector" if t < 3 else "scalar", eg[0][:, t, :], ye[:, t, :], half_of(gc_t, 0))
        sum_rows(1)
        for t in range(PACK):
            gather("scalar", eg[1][:, t, :], ye[:, t, :], half_of(gc_t, 1))
        sum_cols(0)
        nc.vector.quantize_mx(
            out=hid_w[:].bitcast(FP8X4), scales=hid_s[:], in_=hid[:].rearrange("p s m t -> p (s m t)")
        )
        quant_cols(0)
        second_product(0)
        for s in range(PACK):
            negate(s, 0)
        sum_cols(1)
        quant_cols(1)
        second_product(1)

        for s in range(PACK):
            negate(s, 1)
            means(s)
        for s in range(PACK):
            spread(s)
        late = keep.tile([P, PACK * S - EARLY_COLS], F32, name="late", tag="dev", align_bytes=64)

        def paired(s, cols):
            lo, hi = s * S + cols.start, s * S + cols.stop
            return early[:, lo:hi] if hi <= EARLY_COLS else late[:, lo - EARLY_COLS : hi - EARLY_COLS]

        halves = [slice(0, HALF), slice(HALF, S)]
        for s in range(2):
            gather("vector", paired(s, slice(0, S)), neg[:, s * S : s * S + VECTOR_WINDOW], pair_t[:])
        gather("scalar", paired(2, slice(0, S)), neg[:, 2 * S : 2 * S + SCALAR_WINDOW], pair_t[:])
        for h in range(2):
            gather("scalar", paired(3, halves[h]), neg[:, 3 * S :], half_of(pair_t, h))
        steps = [(s, slice(0, S)) for s in range(PACK - 1)] + [(PACK - 1, cols) for cols in halves]
        for n, (s, cols) in enumerate(steps):
            larger(s, cols, paired(s, cols))
            if cols.start == 0:
                nc.vector.reciprocal(inv[s][:], den[s][:])
            if n > 0:
                finish(*steps[n - 1])
        round_cols(nc.scalar.copy, halves[0])
        finish(*steps[-1])
        parts = [slice(HALF, HALF + HALF // 2), slice(HALF + HALF // 2, S)]
        for part in parts:
            round_cols(nc.vector.tensor_copy, part)
        for part in parts:
            quant_out(part)
        store_words(halves[1])
        quant_out(halves[0])
        store_words(halves[0])
        for q in range(4):
            queue = nc.scalar if q % 2 else nc.sync
            queue.dma_start(out_2[0, 4 * q : 4 * q + 4, :].bitcast(I32), res_s[32 * q : 32 * q + 4, :].bitcast(I32))
